import numpy as np
import ml_dtypes


def mxq(x, axis, fmt="e4m3"):
    dtype, down = {"e4m3": (ml_dtypes.float8_e4m3fn, 7), "e5m2": (ml_dtypes.float8_e5m2, 14)}[fmt]
    v = np.moveaxis(np.asarray(x, np.float32).astype(ml_dtypes.bfloat16).astype(np.float64), axis, -1)
    blocks = v.reshape(v.shape[:-1] + (-1, 32))
    amax = np.abs(blocks).max(-1, keepdims=True)
    byte = np.maximum(np.where(amax > 0, np.frexp(amax)[1] - 1 + 127, 0) - down, 1)
    scale = np.exp2(byte - 127.0)
    codes = (blocks / scale).astype(np.float32).astype(dtype).astype(np.float64)
    return np.moveaxis((codes * scale).reshape(v.shape), -1, axis)


WIDE = False


def mx_kscale(k):
    if not WIDE:
        return np.ones(k)
    levels = np.array([10, -10, 5, -5, 0])
    if k % 512:
        return np.exp2(np.random.permutation(np.resize(levels, k // 32))).repeat(32)
    a = np.empty((k // 512, 16))
    for p in range(k // 512):
        a[p, :8] = np.random.permutation(np.resize(levels, 8))
        for g in range(8):
            far = levels[np.abs(levels - a[p, g]) >= 10]
            a[p, g + 8] = far[np.random.randint(len(far))]
    return np.exp2(a.ravel()).repeat(32)


def f64(x):
    return np.asarray(x).astype(np.float64)


def striped(idx):
    return np.tile(np.asarray(idx).reshape(-1, 16).T, (8, 1)).astype(np.uint16)


def unstriped(offs):
    return offs[:16].T.reshape(-1).astype(np.int64)


E2M1 = np.array([0.0, 0.5, 1.0, 1.5, 2.0, 3.0, 4.0, 6.0, -0.0, -0.5, -1.0, -1.5, -2.0, -3.0, -4.0, -6.0])


def pack_weight(w, fmt):
    k, n = w.shape
    w = f64(np.asarray(w, np.float32).astype(ml_dtypes.bfloat16)).reshape(k // 32, 32, n)
    amax = np.abs(w).max(1)
    if fmt == "e4m3":
        byte = np.frexp(amax)[1] - 1 + 127 - 7
    else:
        mant, ex = np.frexp(amax / 6.0)
        byte = np.where(mant > 0.5, ex, ex - 1) + 127
    byte = np.clip(np.where(amax > 0, byte, 1), 1, 254)
    scaled = (w * np.exp2(127.0 - byte)[:, None, :]).reshape(k, n).astype(np.float32)
    by_word = np.ascontiguousarray(scaled.reshape(k // 512, 128, 4, n).transpose(0, 1, 3, 2))
    if fmt == "e4m3":
        words = by_word.astype(ml_dtypes.float8_e4m3fn).view(np.uint8)
    else:
        c = by_word.astype(ml_dtypes.float4_e2m1fn).view(np.uint8) & 0xF
        words = (c[..., 0::2] | (c[..., 1::2] << 4)).reshape(k // 512, 128, 2 * n)
    return np.ascontiguousarray(words), np.ascontiguousarray(byte.astype(np.uint8).reshape(k // 512, 16, n))


def unpack_weight(words, scales, fmt):
    g, _, n = scales.shape
    words = np.ascontiguousarray(words).reshape(g, 128, n, -1)
    if fmt == "e4m3":
        vals = words.view(ml_dtypes.float8_e4m3fn).astype(np.float64)
    else:
        nib = np.empty((g, 128, n, 4), np.uint8)
        nib[..., 0::2] = words & 0xF
        nib[..., 1::2] = words >> 4
        vals = E2M1[nib]
    vals = vals * np.repeat(np.exp2(scales.astype(np.float64) - 127.0), 8, axis=1)[..., None]
    return vals.transpose(0, 1, 3, 2).reshape(g * 512, n)


D, E, T, I, Q = 512, 512, 2048, 512, 128


def setup_inputs():
    n = np.random.standard_normal
    idx = np.random.permutation(T)[:I]
    fd = mx_kscale(D)
    fe = mx_kscale(E)
    keysp = pack_weight(n((D, T)) / fd[:, None], "e2m1")
    valsp = pack_weight(n((E, T)) / fe[:, None], "e2m1")
    return {
        "query": (n((D, Q)) * 0.7 / np.sqrt(D) * fd[:, None]).astype(np.float32),
        "query2": (n((D, Q)) * 0.7 / np.sqrt(D) * fd[:, None]).astype(np.float32),
        "keys_words": keysp[0],
        "keys_scales": keysp[1],
        "gout": (n((E, Q)) * 1 / np.sqrt(E) * fe[:, None]).astype(np.float32),
        "vals_words": valsp[0],
        "vals_scales": valsp[1],
        "size": (np.random.uniform(0.5, 2.0, (1, I))).astype(np.float32),
        "old": (0.5 * n((Q, T))).astype(np.float32),
        "offs": striped(idx),
    }


def reference(query, query2, keys_words, keys_scales, gout, vals_words, vals_scales, size, old, offs):
    idx = unstriped(offs)
    keysu = unpack_weight(keys_words, keys_scales, "e2m1")
    valsu = unpack_weight(vals_words, vals_scales, "e2m1")
    queryq = mxq(f64(query), 0, "e4m3")
    keysidxg = keysu[:, idx]
    a = queryq.T @ keysidxg
    query2q = mxq(f64(query2), 0, "e4m3")
    b = query2q.T @ keysidxg
    pa = np.exp(a - np.max(a, axis=1, keepdims=True))
    wa = pa / np.sum(pa, axis=1, keepdims=True)
    pb = np.exp(b - np.max(b, axis=1, keepdims=True))
    wb = pb / np.sum(pb, axis=1, keepdims=True)
    goutq = mxq(f64(gout), 0, "e4m3")
    valsidxg = valsu[:, idx]
    c0 = goutq.T @ valsidxg
    dwa = c0 * f64(size) / (wa + wb) * wb - c0 * f64(size) * wa * wb / np.square(wa + wb)
    dpa = dwa / np.sum(pa, axis=1, keepdims=True) + np.sum(dwa * pa / np.square(np.sum(pa, axis=1, keepdims=True)) * (-1.0), axis=1, keepdims=True)
    da = dpa * pa
    gs = da * 1024.0
    gf = np.zeros((Q, T))
    gf[:, idx] = gs
    y = f64(old) + gf
    return y

@@ -1,0 +1,198 @@
+import math
+from contextlib import ExitStack
+
+import concourse.mybir as mybir
+
+D, E, T, I, Q = 512, 512, 2048, 512, 128
+FLOPS = 3 * 2 * D * Q * I
+
+F32 = mybir.dt.float32
+BF16 = mybir.dt.bfloat16
+I32 = mybir.dt.int32
+U32 = mybir.dt.uint32
+U16 = mybir.dt.uint16
+U8 = mybir.dt.uint8
+FP8X4 = mybir.dt.float8_e4m3fn_x4
+FP4X4 = mybir.dt.float4_e2m1fn_x4
+ALU = mybir.AluOpType
+ACT = mybir.ActivationFunctionType
+
+P = 128
+PACK = 4
+TERMS = 12
+LN2_PER_BIT = math.log(2.0) / 2.0**23
+CHUNKS = [512, 512, 512, 512]
+
+
+def tile_attend_bagreement_s_kernel(
+    tc, query, query2, keys_words, keys_scales, gout, vals_words, vals_scales, size, old, offs, out
+):
+    nc = tc.nc
+    with ExitStack() as ctx:
+        sb = ctx.enter_context(tc.tile_pool(name="sb", bufs=1))
+        ps = ctx.enter_context(tc.psum_pool(name="ps", bufs=1))
+
+        def tile(name, shape, dtype):
+            return sb.tile(shape, dtype, name=name, align_bytes=64)
+
+        offsets = tile("offsets", [P, I // 16], U16)
+        kw = tile("kw", [P, T], U16)
+        vw = tile("vw", [P, T], U16)
+        ks = tile("ks", [P, T], U8)
+        vs = tile("vs", [P, T], U8)
+        raw = [tile("raw%d" % j, [P, PACK, Q], F32) for j in range(2)]
+        raw.append(sb.tile([P, PACK, Q], F32, name="raw2", tag="neg_a", align_bytes=64))
+        size_b = tile("size_b", [P, I], F32)
+        old_sb = tile("old_sb", [P, T], F32)
+        gf = tile("gf", [P, T], F32)
+
+        def load_scales(queue, dst, src):
+            rows = src[0].bitcast(I32)
+            for quad in range(4):
+                queue.dma_start(
+                    out=dst[32 * quad : 32 * quad + 4, :].bitcast(I32), in_=rows[4 * quad : 4 * quad + 4, :]
+                )
+
+        def load_rows(queue, dst, src):
+            queue.dma_start(out=dst[:], in_=src.rearrange("(p j) q -> p j q", j=PACK))
+
+        nc.vector.memset(ks[:].bitcast(I32), 0)
+        nc.gpsimd.memset(vs[:].bitcast(I32), 0)
+        nc.sync.dma_start(offsets[:], offs)
+        load_rows(nc.scalar, raw[0], query)
+        load_rows(nc.scalar, raw[1], query2)
+        load_scales(nc.sync, ks, keys_scales)
+        nc.sync.dma_start(out=kw[:].bitcast(I32), in_=keys_words[0].bitcast(I32))
+        load_scales(nc.sync, vs, vals_scales)
+        load_rows(nc.sync, raw[2], gout)
+        nc.sync.dma_start(out=vw[:].bitcast(I32), in_=vals_words[0].bitcast(I32))
+        nc.sync.dma_start(out=size_b[:], in_=size.partition_broadcast(P))
+        nc.sync.dma_start(out=old_sb[:], in_=old)
+
+        counts = tile("counts", [P, TERMS - 1], F32)
+        inverses = tile("inverses", [P, TERMS - 1], F32)
+        series = tile("series", [P, TERMS], F32)
+        nc.gpsimd.iota(
+            counts[:], [[-1, TERMS - 1]], base=TERMS - 1, channel_multiplier=0, allow_small_or_imprecise_dtypes=True
+        )
+        nc.vector.reciprocal(inverses[:], counts[:])
+        nc.scalar.activation(series[:, 0 : TERMS - 1 : 2], inverses[:, 0 : TERMS - 1 : 2], ACT.Copy, scale=-0.5)
+        nc.scalar.activation(series[:, 1 : TERMS - 1 : 2], inverses[:, 1 : TERMS - 1 : 2], ACT.Copy, scale=0.5)
+        nc.vector.memset(gf[:], 0.0)
+
+        qq_bf = tile("qq_bf", [P, 2, Q, PACK], BF16)
+        g_bf = tile("g_bf", [P, Q, PACK], BF16)
+        qq_codes = tile("qq_codes", [P, 2 * Q], U32)
+        qq_scales = tile("qq_scales", [P, 2 * Q], U8)
+        g_codes = tile("g_codes", [P, Q], U32)
+        g_scales = tile("g_scales", [P, Q], U8)
+        nc.scalar.activation(qq_bf[:, 0], raw[0][:].rearrange("p j q -> p q j"), ACT.Copy)
+        nc.scalar.activation(qq_bf[:, 1], raw[1][:].rearrange("p j q -> p q j"), ACT.Copy)
+        nc.scalar.activation(g_bf[:], raw[2][:].rearrange("p j q -> p q j"), ACT.Copy)
+
+        kwg = tile("kwg", [P, I], U16)
+        ksg = tile("ksg", [P, I], U8)
+        vsg = tile("vsg", [P, I], U8)
+        a_ps = ps.tile([P, I], F32, name="a_ps")
+        b_ps = ps.tile([P, I], F32, name="b_ps")
+        c_ps = ps.tile([P, I], F32, name="c_ps")
+
+        nc.vector.tensor_copy(ksg[:], ks[:].indirect(offsets[:]))
+        nc.vector.tensor_copy(kwg[:], kw[:].indirect(offsets[:]))
+        nc.vector.quantize_mx(
+            out=qq_codes[:].bitcast(FP8X4), scales=qq_scales[:], in_=qq_bf[:].rearrange("p s q j -> p (s q j)")
+        )
+        for s, bank in enumerate((a_ps, b_ps)):
+            nc.tensor.matmul_mx(
+                out=bank[:],
+                lhsT=qq_codes[:, s * Q : (s + 1) * Q].bitcast(FP8X4),
+                lhsT_scale=qq_scales[:, s * Q : (s + 1) * Q],
+                rhs=kwg[:].bitcast(FP4X4),
+                rhs_scale=ksg[:],
+                start=True,
+                stop=True,
+            )
+        nc.vector.tensor_copy(vsg[:], vs[:].indirect(offsets[:]))
+
+        def column(name):
+            return tile(name, [P, 1], F32)
+
+        neg_a = sb.tile([P, I], F32, name="neg_a", tag="neg_a", align_bytes=64)
+        neg_max_a = column("neg_max_a")
+        neg_max_b = column("neg_max_b")
+        pa = tile("pa", [P, I], F32)
+        pb = tile("pb", [P, I], F32)
+        sum_a = column("sum_a")
+        sum_b = column("sum_b")
+        nc.vector.tensor_scalar(neg_a[:], a_ps[:], -1.0, None, ALU.mult, ALU.min, accum_out=neg_max_a[:])
+        nc.scalar.activation(pa[:], neg_a[:], ACT.Exp, bias=neg_max_a[:], scale=-1.0, accum_out=sum_a[:])
+        nc.vector.tensor_reduce(neg_max_b[:], b_ps[:], mybir.AxisListType.X, ALU.max, negate=True)
+        nc.scalar.activation(pb[:], b_ps[:], ACT.Exp, bias=neg_max_b[:], accum_out=sum_b[:])
+
+        gap = column("gap")
+        inv_a = column("inv_a")
+        neg_inv_a = column("neg_inv_a")
+        guess_a = column("guess_a")
+        half_guess_a = column("half_guess_a")
+        ratio = column("ratio")
+        undo = column("undo")
+        rest = tile("rest", [P, TERMS], F32)
+        horner = tile("horner", [P, TERMS], F32)
+        diff = tile("diff", [P, I], F32)
+        nc.vector.quantize_mx(
+            out=g_codes[:].bitcast(FP8X4), scales=g_scales[:], in_=g_bf[:].rearrange("p q j -> p (q j)")
+        )
+        nc.vector.tensor_tensor(gap[:], neg_max_b[:], neg_max_a[:], ALU.subtract)
+        nc.vector.reciprocal(inv_a[:], sum_a[:])
+        nc.vector.scalar_tensor_tensor(diff[:], b_ps[:], gap[:], neg_a[:], ALU.add, ALU.add)
+
+        vwg = sb.tile([P, I], U16, name="vwg", tag="neg_a", align_bytes=64)
+        nc.vector.tensor_copy(vwg[:], vw[:].indirect(offsets[:]))
+        nc.tensor.matmul_mx(
+            out=c_ps[:],
+            lhsT=g_codes[:].bitcast(FP8X4),
+            lhsT_scale=g_scales[:],
+            rhs=vwg[:].bitcast(FP4X4),
+            rhs_scale=vsg[:],
+            start=True,
+            stop=True,
+        )
+
+        nc.scalar.activation(guess_a[:], sum_a[:].bitcast(U32), ACT.Copy, scale=LN2_PER_BIT)
+        nc.scalar.activation(half_guess_a[:], sum_a[:].bitcast(U32), ACT.Copy, scale=0.5 * LN2_PER_BIT)
+        nc.scalar.activation(undo[:], sum_b[:].bitcast(U32), ACT.Exp, bias=guess_a[:], scale=-LN2_PER_BIT)
+        nc.scalar.activation(ratio[:], sum_b[:], ACT.Copy, scale=inv_a[:])
+        nc.scalar.activation(
+            series[:, TERMS - 1 :],
+            sum_b[:].bitcast(U32),
+            ACT.Identity,
+            bias=half_guess_a[:],
+            scale=-0.5 * LN2_PER_BIT,
+        )
+        nc.scalar.activation(rest[:], undo[:].to_broadcast([P, TERMS]), ACT.Identity, bias=-1.0, scale=ratio[:])
+        nc.scalar.activation(neg_inv_a[:], inv_a[:], ACT.Copy, scale=-1.0)
+        nc.vector.tensor_tensor_scan(horner[:], rest[:], series[:], 0.5 / TERMS, ALU.mult, ALU.add)
+
+        tanh = tile("tanh", [P, I], F32)
+        share2 = tile("share2", [P, I], F32)
+        nc.scalar.activation(tanh[:], diff[:], ACT.Tanh, bias=horner[:, TERMS - 1 :], scale=0.5)
+        nc.scalar.activation(share2[:], tanh[:], ACT.Square, bias=0.5, scale=0.5)
+
+        sized = tile("sized", [P, I], F32)
+        cw = tile("cw", [P, I], F32)
+        first = tile("first", [P, I], F32)
+        second = tile("second", [P, I], F32)
+        total = column("total")
+        nc.vector.scalar_tensor_tensor(sized[:], pa[:], inv_a[:], size_b[:], ALU.mult, ALU.mult)
+        nc.vector.tensor_tensor(cw[:], c_ps[:], sized[:], ALU.mult)
+        nc.vector.scalar_tensor_tensor(first[:], share2[:], 1024.0, cw[:], ALU.mult, ALU.mult, accum_out=total[:])
+        nc.vector.tensor_scalar(second[:], pa[:], total[:], neg_inv_a[:], ALU.mult, ALU.mult)
+        nc.vector.tensor_tensor(gf[:].indirect(offsets[:]), first[:], second[:], ALU.add)
+
+        start = 0
+        for n, width in enumerate(CHUNKS):
+            cols = slice(start, start + width)
+            y = tile("y%d" % n, [P, width], F32)
+            nc.vector.tensor_tensor(y[:], gf[:, cols], old_sb[:, cols], ALU.add)
+            (nc.sync if n % 2 == 0 else nc.scalar).dma_start(out=out[:, cols], in_=y[:])
+            start = start + width

@@ -2,6 +2,7 @@ import math
 from contextlib import ExitStack
 
 import concourse.mybir as mybir
+from concourse.masks import make_identity
 
 D, E, T, I, Q = 512, 512, 2048, 512, 128
 FLOPS = 3 * 2 * D * Q * I
@@ -21,7 +22,8 @@ P = 128
 PACK = 4
 TERMS = 12
 LN2_PER_BIT = math.log(2.0) / 2.0**23
-CHUNKS = [512, 512, 512, 512]
+CHUNKS = [256, 512, 512, 512, 256]
+HALVES = [slice(0, I // 2), slice(I // 2, I)]
 
 
 def tile_attend_bagreement_s_kernel(
@@ -32,63 +34,84 @@ def tile_attend_bagreement_s_kernel(
         sb = ctx.enter_context(tc.tile_pool(name="sb", bufs=1))
         ps = ctx.enter_context(tc.psum_pool(name="ps", bufs=1))
 
-        def tile(name, shape, dtype):
-            return sb.tile(shape, dtype, name=name, align_bytes=64)
+        def tile(name, shape, dtype, tag=""):
+            return sb.tile(shape, dtype, name=name, tag=tag or name, align_bytes=64)
 
-        offsets = tile("offsets", [P, I // 16], U16)
-        kw = tile("kw", [P, T], U16)
-        vw = tile("vw", [P, T], U16)
-        ks = tile("ks", [P, T], U8)
-        vs = tile("vs", [P, T], U8)
-        raw = [tile("raw%d" % j, [P, PACK, Q], F32) for j in range(2)]
-        raw.append(sb.tile([P, PACK, Q], F32, name="raw2", tag="neg_a", align_bytes=64))
-        size_b = tile("size_b", [P, I], F32)
-        old_sb = tile("old_sb", [P, T], F32)
-        gf = tile("gf", [P, T], F32)
+        def column(name):
+            return tile(name, [P, 1], F32)
 
-        def load_scales(queue, dst, src):
+        def load_scales(dst, src):
             rows = src[0].bitcast(I32)
             for quad in range(4):
-                queue.dma_start(
+                nc.sync.dma_start(
                     out=dst[32 * quad : 32 * quad + 4, :].bitcast(I32), in_=rows[4 * quad : 4 * quad + 4, :]
                 )
 
-        def load_rows(queue, dst, src):
-            queue.dma_start(out=dst[:], in_=src.rearrange("(p j) q -> p j q", j=PACK))
+        def load_words(dst, src):
+            nc.sync.dma_start(out=dst[:].bitcast(I32), in_=src[0].bitcast(I32))
 
-        nc.vector.memset(ks[:].bitcast(I32), 0)
-        nc.gpsimd.memset(vs[:].bitcast(I32), 0)
+        def load_rows(dst, src):
+            nc.sync.dma_start(out=dst[:], in_=src.rearrange("(p j) q -> p j q", j=PACK))
+
+        offsets = tile("offsets", [P, I // 16], U16)
+        ks = tile("ks", [P, T], U8)
+        ones = tile("ones", [P, TERMS - 1], F32)
+        twos = tile("twos", [P, TERMS - 1], F32)
+        top = column("top")
+        identity = tile("identity", [P, P], F32)
+        nc.gpsimd.memset(ks[:].bitcast(I32), 0)
+        nc.gpsimd.memset(ones[:], 1.0)
+        nc.gpsimd.memset(twos[:], 2.0)
+        nc.gpsimd.memset(top[:], 2.0 * TERMS)
+        make_identity(nc, identity[:])
         nc.sync.dma_start(offsets[:], offs)
-        load_rows(nc.scalar, raw[0], query)
-        load_rows(nc.scalar, raw[1], query2)
-        load_scales(nc.sync, ks, keys_scales)
-        nc.sync.dma_start(out=kw[:].bitcast(I32), in_=keys_words[0].bitcast(I32))
-        load_scales(nc.sync, vs, vals_scales)
-        load_rows(nc.sync, raw[2], gout)
-        nc.sync.dma_start(out=vw[:].bitcast(I32), in_=vals_words[0].bitcast(I32))
-        nc.sync.dma_start(out=size_b[:], in_=size.partition_broadcast(P))
-        nc.sync.dma_start(out=old_sb[:], in_=old)
+        load_scales(ks, keys_scales)
 
         counts = tile("counts", [P, TERMS - 1], F32)
         inverses = tile("inverses", [P, TERMS - 1], F32)
         series = tile("series", [P, TERMS], F32)
-        nc.gpsimd.iota(
-            counts[:], [[-1, TERMS - 1]], base=TERMS - 1, channel_multiplier=0, allow_small_or_imprecise_dtypes=True
-        )
+        nc.vector.tensor_tensor_scan(counts[:], ones[:], twos[:], top[:], ALU.mult, ALU.subtract)
         nc.vector.reciprocal(inverses[:], counts[:])
-        nc.scalar.activation(series[:, 0 : TERMS - 1 : 2], inverses[:, 0 : TERMS - 1 : 2], ACT.Copy, scale=-0.5)
-        nc.scalar.activation(series[:, 1 : TERMS - 1 : 2], inverses[:, 1 : TERMS - 1 : 2], ACT.Copy, scale=0.5)
-        nc.vector.memset(gf[:], 0.0)
+        nc.scalar.activation(series[:, 0 : TERMS - 1 : 2], inverses[:, 0 : TERMS - 1 : 2], ACT.Copy, scale=-1.0)
+        nc.scalar.activation(series[:, 1 : TERMS - 1 : 2], inverses[:, 1 : TERMS - 1 : 2], ACT.Copy)
 
-        qq_bf = tile("qq_bf", [P, 2, Q, PACK], BF16)
-        g_bf = tile("g_bf", [P, Q, PACK], BF16)
-        qq_codes = tile("qq_codes", [P, 2 * Q], U32)
-        qq_scales = tile("qq_scales", [P, 2 * Q], U8)
-        g_codes = tile("g_codes", [P, Q], U32)
-        g_scales = tile("g_scales", [P, Q], U8)
-        nc.scalar.activation(qq_bf[:, 0], raw[0][:].rearrange("p j q -> p q j"), ACT.Copy)
-        nc.scalar.activation(qq_bf[:, 1], raw[1][:].rearrange("p j q -> p q j"), ACT.Copy)
-        nc.scalar.activation(g_bf[:], raw[2][:].rearrange("p j q -> p q j"), ACT.Copy)
+        kw = tile("kw", [P, T], U16, tag="ones")
+        load_words(kw, keys_words)
+        qa_raw = tile("qa_raw", [P, PACK, Q], F32, tag="top")
+        load_rows(qa_raw, query)
+        vs = tile("vs", [P, T], U8, tag="twos")
+        nc.vector.memset(vs[:].bitcast(I32), 0)
+        load_scales(vs, vals_scales)
+        gf = tile("gf", [P, T], F32, tag="counts")
+        nc.vector.memset(gf[:], 0.0)
+        qb_raw = tile("qb_raw", [P, PACK, Q], F32, tag="inverses")
+        load_rows(qb_raw, query2)
+
+        bf = [tile("bf%d" % s, [P, Q, PACK], BF16) for s in range(3)]
+        codes = [tile("codes%d" % s, [P, Q], U32) for s in range(3)]
+        scales = [tile("scales%d" % s, [P, Q], U8) for s in range(3)]
+
+        def cast(s, raw):
+            nc.scalar.activation(bf[s][:], raw[:].rearrange("p j q -> p q j"), ACT.Copy)
+
+        cast(0, qa_raw)
+        cast(1, qb_raw)
+
+        def quantise(s):
+            nc.vector.quantize_mx(
+                out=codes[s][:].bitcast(FP8X4), scales=scales[s][:], in_=bf[s][:].rearrange("p q j -> p (q j)")
+            )
+
+        def product(bank, s, words, word_scales):
+            nc.tensor.matmul_mx(
+                out=bank[:],
+                lhsT=codes[s][:].bitcast(FP8X4),
+                lhsT_scale=scales[s][:],
+                rhs=words[:].bitcast(FP4X4),
+                rhs_scale=word_scales[:],
+                start=True,
+                stop=True,
+            )
 
         kwg = tile("kwg", [P, I], U16)
         ksg = tile("ksg", [P, I], U8)
@@ -98,38 +121,40 @@ def tile_attend_bagreement_s_kernel(
         c_ps = ps.tile([P, I], F32, name="c_ps")
 
         nc.vector.tensor_copy(ksg[:], ks[:].indirect(offsets[:]))
+        g_raw = tile("g_raw", [P, PACK, Q], F32, tag="ks")
+        load_rows(g_raw, gout)
+        cast(2, g_raw)
         nc.vector.tensor_copy(kwg[:], kw[:].indirect(offsets[:]))
-        nc.vector.quantize_mx(
-            out=qq_codes[:].bitcast(FP8X4), scales=qq_scales[:], in_=qq_bf[:].rearrange("p s q j -> p (s q j)")
-        )
-        for s, bank in enumerate((a_ps, b_ps)):
-            nc.tensor.matmul_mx(
-                out=bank[:],
-                lhsT=qq_codes[:, s * Q : (s + 1) * Q].bitcast(FP8X4),
-                lhsT_scale=qq_scales[:, s * Q : (s + 1) * Q],
-                rhs=kwg[:].bitcast(FP4X4),
-                rhs_scale=ksg[:],
-                start=True,
-                stop=True,
-            )
+        vw = tile("vw", [P, T], U16, tag="ones")
+        load_words(vw, vals_words)
+        size_cols = tile("size_cols", [P, PACK], F32, tag="top")
+        nc.sync.dma_start(out=size_cols[:], in_=size.rearrange("o (p j) -> (o p) j", j=PACK))
+        quantise(0)
+        old_sb = tile("old_sb", [P, T], F32, tag="bf0")
+        nc.sync.dma_start(out=old_sb[:], in_=old)
+        product(a_ps, 0, kwg, ksg)
         nc.vector.tensor_copy(vsg[:], vs[:].indirect(offsets[:]))
+        quantise(1)
+        product(b_ps, 1, kwg, ksg)
 
-        def column(name):
-            return tile(name, [P, 1], F32)
+        size_ps = ps.tile([P, PACK, P], F32, name="size_ps")
+        for j in range(PACK):
+            nc.tensor.transpose(size_ps[:, j, :], size_cols[:, j : j + 1].to_broadcast([P, P]), identity[:])
 
-        neg_a = sb.tile([P, I], F32, name="neg_a", tag="neg_a", align_bytes=64)
+        neg_a = tile("neg_a", [P, I], F32, tag="inverses")
+        neg_b = tile("neg_b", [P, I], F32)
         neg_max_a = column("neg_max_a")
         neg_max_b = column("neg_max_b")
-        pa = tile("pa", [P, I], F32)
+        pa = tile("pa", [P, I], F32, tag="ks")
         pb = tile("pb", [P, I], F32)
         sum_a = column("sum_a")
         sum_b = column("sum_b")
         nc.vector.tensor_scalar(neg_a[:], a_ps[:], -1.0, None, ALU.mult, ALU.min, accum_out=neg_max_a[:])
         nc.scalar.activation(pa[:], neg_a[:], ACT.Exp, bias=neg_max_a[:], scale=-1.0, accum_out=sum_a[:])
-        nc.vector.tensor_reduce(neg_max_b[:], b_ps[:], mybir.AxisListType.X, ALU.max, negate=True)
-        nc.scalar.activation(pb[:], b_ps[:], ACT.Exp, bias=neg_max_b[:], accum_out=sum_b[:])
+        nc.vector.tensor_scalar(neg_b[:], b_ps[:], -1.0, None, ALU.mult, ALU.min, accum_out=neg_max_b[:])
+        nc.scalar.activation(pb[:], neg_b[:], ACT.Exp, bias=neg_max_b[:], scale=-1.0, accum_out=sum_b[:])
 
-        gap = column("gap")
+        half_gap = column("half_gap")
         inv_a = column("inv_a")
         neg_inv_a = column("neg_inv_a")
         guess_a = column("guess_a")
@@ -139,27 +164,19 @@ def tile_attend_bagreement_s_kernel(
         rest = tile("rest", [P, TERMS], F32)
         horner = tile("horner", [P, TERMS], F32)
         diff = tile("diff", [P, I], F32)
-        nc.vector.quantize_mx(
-            out=g_codes[:].bitcast(FP8X4), scales=g_scales[:], in_=g_bf[:].rearrange("p q j -> p (q j)")
-        )
-        nc.vector.tensor_tensor(gap[:], neg_max_b[:], neg_max_a[:], ALU.subtract)
+        nc.gpsimd.tensor_scalar(half_gap[:], neg_max_b[:], neg_max_a[:], 0.5, ALU.subtract, ALU.mult)
+        nc.vector.tensor_tensor(diff[:], b_ps[:], neg_a[:], ALU.add)
         nc.vector.reciprocal(inv_a[:], sum_a[:])
-        nc.vector.scalar_tensor_tensor(diff[:], b_ps[:], gap[:], neg_a[:], ALU.add, ALU.add)
+        quantise(2)
 
-        vwg = sb.tile([P, I], U16, name="vwg", tag="neg_a", align_bytes=64)
+        vwg = tile("vwg", [P, I], U16, tag="inverses")
         nc.vector.tensor_copy(vwg[:], vw[:].indirect(offsets[:]))
-        nc.tensor.matmul_mx(
-            out=c_ps[:],
-            lhsT=g_codes[:].bitcast(FP8X4),
-            lhsT_scale=g_scales[:],
-            rhs=vwg[:].bitcast(FP4X4),
-            rhs_scale=vsg[:],
-            start=True,
-            stop=True,
-        )
+        product(c_ps, 2, vwg, vsg)
 
         nc.scalar.activation(guess_a[:], sum_a[:].bitcast(U32), ACT.Copy, scale=LN2_PER_BIT)
-        nc.scalar.activation(half_guess_a[:], sum_a[:].bitcast(U32), ACT.Copy, scale=0.5 * LN2_PER_BIT)
+        nc.scalar.activation(
+            half_guess_a[:], sum_a[:].bitcast(U32), ACT.Identity, bias=half_gap[:], scale=0.5 * LN2_PER_BIT
+        )
         nc.scalar.activation(undo[:], sum_b[:].bitcast(U32), ACT.Exp, bias=guess_a[:], scale=-LN2_PER_BIT)
         nc.scalar.activation(ratio[:], sum_b[:], ACT.Copy, scale=inv_a[:])
         nc.scalar.activation(
@@ -178,13 +195,23 @@ def tile_attend_bagreement_s_kernel(
         nc.scalar.activation(tanh[:], diff[:], ACT.Tanh, bias=horner[:, TERMS - 1 :], scale=0.5)
         nc.scalar.activation(share2[:], tanh[:], ACT.Square, bias=0.5, scale=0.5)
 
-        sized = tile("sized", [P, I], F32)
+        sized = tile("sized", [P, I], F32, tag="undo")
         cw = tile("cw", [P, I], F32)
         first = tile("first", [P, I], F32)
         second = tile("second", [P, I], F32)
         total = column("total")
-        nc.vector.scalar_tensor_tensor(sized[:], pa[:], inv_a[:], size_b[:], ALU.mult, ALU.mult)
-        nc.vector.tensor_tensor(cw[:], c_ps[:], sized[:], ALU.mult)
+        size_row = size_ps[:].rearrange("p j n -> p n j")
+        for h, cols in enumerate(HALVES):
+            nc.vector.scalar_tensor_tensor(
+                sized[:, cols].rearrange("p (n j) -> p n j", j=PACK),
+                pa[:, cols].rearrange("p (n j) -> p n j", j=PACK),
+                inv_a[:],
+                size_row[:, h * P // 2 : (h + 1) * P // 2, :],
+                ALU.mult,
+                ALU.mult,
+            )
+        for cols in HALVES:
+            nc.vector.tensor_tensor(cw[:, cols], c_ps[:, cols], sized[:, cols], ALU.mult)
         nc.vector.scalar_tensor_tensor(first[:], share2[:], 1024.0, cw[:], ALU.mult, ALU.mult, accum_out=total[:])
         nc.vector.tensor_scalar(second[:], pa[:], total[:], neg_inv_a[:], ALU.mult, ALU.mult)
         nc.vector.tensor_tensor(gf[:].indirect(offsets[:]), first[:], second[:], ALU.add)

@@ -68,12 +68,14 @@ def tile_attend_bagreement_s_kernel(
         load_scales(ks, keys_scales)
 
         counts = tile("counts", [P, TERMS - 1], F32)
-        inverses = tile("inverses", [P, TERMS - 1], F32)
+        odd = tile("odd", [P, TERMS // 2], F32)
+        even = tile("even", [P, TERMS // 2 - 1], F32)
         series = tile("series", [P, TERMS], F32)
         nc.vector.tensor_tensor_scan(counts[:], ones[:], twos[:], top[:], ALU.mult, ALU.subtract)
-        nc.vector.reciprocal(inverses[:], counts[:])
-        nc.scalar.activation(series[:, 0 : TERMS - 1 : 2], inverses[:, 0 : TERMS - 1 : 2], ACT.Copy, scale=-1.0)
-        nc.scalar.activation(series[:, 1 : TERMS - 1 : 2], inverses[:, 1 : TERMS - 1 : 2], ACT.Copy)
+        nc.vector.reciprocal(odd[:], counts[:, 0 : TERMS - 1 : 2])
+        nc.vector.reciprocal(even[:], counts[:, 1 : TERMS - 1 : 2])
+        nc.scalar.activation(series[:, 0 : TERMS - 1 : 2], odd[:], ACT.Copy, scale=-1.0)
+        nc.scalar.activation(series[:, 1 : TERMS - 1 : 2], even[:], ACT.Copy)
 
         kw = tile("kw", [P, T], U16, tag="ones")
         load_words(kw, keys_words)
@@ -84,8 +86,10 @@ def tile_attend_bagreement_s_kernel(
         load_scales(vs, vals_scales)
         gf = tile("gf", [P, T], F32, tag="counts")
         nc.vector.memset(gf[:], 0.0)
-        qb_raw = tile("qb_raw", [P, PACK, Q], F32, tag="inverses")
+        qb_raw = tile("qb_raw", [P, PACK, Q], F32, tag="odd")
         load_rows(qb_raw, query2)
+        g_raw = tile("g_raw", [P, PACK, Q], F32, tag="even")
+        load_rows(g_raw, gout)
 
         bf = [tile("bf%d" % s, [P, Q, PACK], BF16) for s in range(3)]
         codes = [tile("codes%d" % s, [P, Q], U32) for s in range(3)]
@@ -96,6 +100,7 @@ def tile_attend_bagreement_s_kernel(
 
         cast(0, qa_raw)
         cast(1, qb_raw)
+        cast(2, g_raw)
 
         def quantise(s):
             nc.vector.quantize_mx(
@@ -121,12 +126,9 @@ def tile_attend_bagreement_s_kernel(
         c_ps = ps.tile([P, I], F32, name="c_ps")
 
         nc.vector.tensor_copy(ksg[:], ks[:].indirect(offsets[:]))
-        g_raw = tile("g_raw", [P, PACK, Q], F32, tag="ks")
-        load_rows(g_raw, gout)
-        cast(2, g_raw)
-        nc.vector.tensor_copy(kwg[:], kw[:].indirect(offsets[:]))
-        vw = tile("vw", [P, T], U16, tag="ones")
+        vw = tile("vw", [P, T], U16, tag="ks")
         load_words(vw, vals_words)
+        nc.vector.tensor_copy(kwg[:], kw[:].indirect(offsets[:]))
         size_cols = tile("size_cols", [P, PACK], F32, tag="top")
         nc.sync.dma_start(out=size_cols[:], in_=size.rearrange("o (p j) -> (o p) j", j=PACK))
         quantise(0)
@@ -141,11 +143,11 @@ def tile_attend_bagreement_s_kernel(
         for j in range(PACK):
             nc.tensor.transpose(size_ps[:, j, :], size_cols[:, j : j + 1].to_broadcast([P, P]), identity[:])
 
-        neg_a = tile("neg_a", [P, I], F32, tag="inverses")
+        neg_a = tile("neg_a", [P, I], F32, tag="odd")
         neg_b = tile("neg_b", [P, I], F32)
         neg_max_a = column("neg_max_a")
         neg_max_b = column("neg_max_b")
-        pa = tile("pa", [P, I], F32, tag="ks")
+        pa = tile("pa", [P, I], F32, tag="even")
         pb = tile("pb", [P, I], F32)
         sum_a = column("sum_a")
         sum_b = column("sum_b")
@@ -169,7 +171,7 @@ def tile_attend_bagreement_s_kernel(
         nc.vector.reciprocal(inv_a[:], sum_a[:])
         quantise(2)
 
-        vwg = tile("vwg", [P, I], U16, tag="inverses")
+        vwg = tile("vwg", [P, I], U16, tag="odd")
         nc.vector.tensor_copy(vwg[:], vw[:].indirect(offsets[:]))
         product(c_ps, 2, vwg, vsg)
 

import math
from contextlib import ExitStack

import concourse.mybir as mybir
from concourse.masks import make_identity

D, E, T, I, Q = 512, 512, 2048, 512, 128
FLOPS = 3 * 2 * D * Q * I

F32 = mybir.dt.float32
BF16 = mybir.dt.bfloat16
I32 = mybir.dt.int32
U32 = mybir.dt.uint32
U16 = mybir.dt.uint16
U8 = mybir.dt.uint8
FP8X4 = mybir.dt.float8_e4m3fn_x4
FP4X4 = mybir.dt.float4_e2m1fn_x4
ALU = mybir.AluOpType
ACT = mybir.ActivationFunctionType

P = 128
PACK = 4
TERMS = 12
LN2_PER_BIT = math.log(2.0) / 2.0**23
CHUNKS = [256, 512, 512, 512, 256]
HALVES = [slice(0, I // 2), slice(I // 2, I)]


def tile_attend_bagreement_s_kernel(
    tc, query, query2, keys_words, keys_scales, gout, vals_words, vals_scales, size, old, offs, out
):
    nc = tc.nc
    with ExitStack() as ctx:
        sb = ctx.enter_context(tc.tile_pool(name="sb", bufs=1))
        ps = ctx.enter_context(tc.psum_pool(name="ps", bufs=1))

        def tile(name, shape, dtype, tag=""):
            return sb.tile(shape, dtype, name=name, tag=tag or name, align_bytes=64)

        def column(name):
            return tile(name, [P, 1], F32)

        def load_scales(dst, src):
            rows = src[0].bitcast(I32)
            for quad in range(4):
                nc.sync.dma_start(
                    out=dst[32 * quad : 32 * quad + 4, :].bitcast(I32), in_=rows[4 * quad : 4 * quad + 4, :]
                )

        def load_words(dst, src):
            nc.sync.dma_start(out=dst[:].bitcast(I32), in_=src[0].bitcast(I32))

        def load_rows(dst, src):
            nc.sync.dma_start(out=dst[:], in_=src.rearrange("(p j) q -> p j q", j=PACK))

        offsets = tile("offsets", [P, I // 16], U16)
        ks = tile("ks", [P, T], U8)
        ones = tile("ones", [P, TERMS - 1], F32)
        twos = tile("twos", [P, TERMS - 1], F32)
        top = column("top")
        identity = tile("identity", [P, P], F32)
        nc.gpsimd.memset(ks[:].bitcast(I32), 0)
        nc.gpsimd.memset(ones[:], 1.0)
        nc.gpsimd.memset(twos[:], 2.0)
        nc.gpsimd.memset(top[:], 2.0 * TERMS)
        make_identity(nc, identity[:])
        nc.sync.dma_start(offsets[:], offs)
        load_scales(ks, keys_scales)

        counts = tile("counts", [P, TERMS - 1], F32)
        odd = tile("odd", [P, TERMS // 2], F32)
        even = tile("even", [P, TERMS // 2 - 1], F32)
        series = tile("series", [P, TERMS], F32)
        nc.vector.tensor_tensor_scan(counts[:], ones[:], twos[:], top[:], ALU.mult, ALU.subtract)
        nc.vector.reciprocal(odd[:], counts[:, 0 : TERMS - 1 : 2])
        nc.vector.reciprocal(even[:], counts[:, 1 : TERMS - 1 : 2])
        nc.scalar.activation(series[:, 0 : TERMS - 1 : 2], odd[:], ACT.Copy, scale=-1.0)
        nc.scalar.activation(series[:, 1 : TERMS - 1 : 2], even[:], ACT.Copy)

        kw = tile("kw", [P, T], U16, tag="ones")
        load_words(kw, keys_words)
        qa_raw = tile("qa_raw", [P, PACK, Q], F32, tag="top")
        load_rows(qa_raw, query)
        vs = tile("vs", [P, T], U8, tag="twos")
        nc.vector.memset(vs[:].bitcast(I32), 0)
        load_scales(vs, vals_scales)
        gf = tile("gf", [P, T], F32, tag="counts")
        nc.vector.memset(gf[:], 0.0)
        qb_raw = tile("qb_raw", [P, PACK, Q], F32, tag="odd")
        load_rows(qb_raw, query2)
        g_raw = tile("g_raw", [P, PACK, Q], F32, tag="even")
        load_rows(g_raw, gout)

        bf = [tile("bf%d" % s, [P, Q, PACK], BF16) for s in range(3)]
        codes = [tile("codes%d" % s, [P, Q], U32) for s in range(3)]
        scales = [tile("scales%d" % s, [P, Q], U8) for s in range(3)]

        def cast(s, raw):
            nc.scalar.activation(bf[s][:], raw[:].rearrange("p j q -> p q j"), ACT.Copy)

        cast(0, qa_raw)
        cast(1, qb_raw)
        cast(2, g_raw)

        def quantise(s):
            nc.vector.quantize_mx(
                out=codes[s][:].bitcast(FP8X4), scales=scales[s][:], in_=bf[s][:].rearrange("p q j -> p (q j)")
            )

        def product(bank, s, words, word_scales):
            nc.tensor.matmul_mx(
                out=bank[:],
                lhsT=codes[s][:].bitcast(FP8X4),
                lhsT_scale=scales[s][:],
                rhs=words[:].bitcast(FP4X4),
                rhs_scale=word_scales[:],
                start=True,
                stop=True,
            )

        kwg = tile("kwg", [P, I], U16)
        ksg = tile("ksg", [P, I], U8)
        vsg = tile("vsg", [P, I], U8)
        a_ps = ps.tile([P, I], F32, name="a_ps")
        b_ps = ps.tile([P, I], F32, name="b_ps")
        c_ps = ps.tile([P, I], F32, name="c_ps")

        nc.vector.tensor_copy(ksg[:], ks[:].indirect(offsets[:]))
        vw = tile("vw", [P, T], U16, tag="ks")
        load_words(vw, vals_words)
        nc.vector.tensor_copy(kwg[:], kw[:].indirect(offsets[:]))
        size_cols = tile("size_cols", [P, PACK], F32, tag="top")
        nc.sync.dma_start(out=size_cols[:], in_=size.rearrange("o (p j) -> (o p) j", j=PACK))
        quantise(0)
        old_sb = tile("old_sb", [P, T], F32, tag="bf0")
        nc.sync.dma_start(out=old_sb[:], in_=old)
        product(a_ps, 0, kwg, ksg)
        nc.vector.tensor_copy(vsg[:], vs[:].indirect(offsets[:]))
        quantise(1)
        product(b_ps, 1, kwg, ksg)

        size_ps = ps.tile([P, PACK, P], F32, name="size_ps")
        for j in range(PACK):
            nc.tensor.transpose(size_ps[:, j, :], size_cols[:, j : j + 1].to_broadcast([P, P]), identity[:])

        neg_a = tile("neg_a", [P, I], F32, tag="odd")
        neg_b = tile("neg_b", [P, I], F32)
        neg_max_a = column("neg_max_a")
        neg_max_b = column("neg_max_b")
        pa = tile("pa", [P, I], F32, tag="even")
        pb = tile("pb", [P, I], F32)
        sum_a = column("sum_a")
        sum_b = column("sum_b")
        nc.vector.tensor_scalar(neg_a[:], a_ps[:], -1.0, None, ALU.mult, ALU.min, accum_out=neg_max_a[:])
        nc.scalar.activation(pa[:], neg_a[:], ACT.Exp, bias=neg_max_a[:], scale=-1.0, accum_out=sum_a[:])
        nc.vector.tensor_scalar(neg_b[:], b_ps[:], -1.0, None, ALU.mult, ALU.min, accum_out=neg_max_b[:])
        nc.scalar.activation(pb[:], neg_b[:], ACT.Exp, bias=neg_max_b[:], scale=-1.0, accum_out=sum_b[:])

        half_gap = column("half_gap")
        inv_a = column("inv_a")
        neg_inv_a = column("neg_inv_a")
        guess_a = column("guess_a")
        half_guess_a = column("half_guess_a")
        ratio = column("ratio")
        undo = column("undo")
        rest = tile("rest", [P, TERMS], F32)
        horner = tile("horner", [P, TERMS], F32)
        diff = tile("diff", [P, I], F32)
        nc.gpsimd.tensor_scalar(half_gap[:], neg_max_b[:], neg_max_a[:], 0.5, ALU.subtract, ALU.mult)
        nc.vector.tensor_tensor(diff[:], b_ps[:], neg_a[:], ALU.add)
        nc.vector.reciprocal(inv_a[:], sum_a[:])
        quantise(2)

        vwg = tile("vwg", [P, I], U16, tag="odd")
        nc.vector.tensor_copy(vwg[:], vw[:].indirect(offsets[:]))
        product(c_ps, 2, vwg, vsg)

        nc.scalar.activation(guess_a[:], sum_a[:].bitcast(U32), ACT.Copy, scale=LN2_PER_BIT)
        nc.scalar.activation(
            half_guess_a[:], sum_a[:].bitcast(U32), ACT.Identity, bias=half_gap[:], scale=0.5 * LN2_PER_BIT
        )
        nc.scalar.activation(undo[:], sum_b[:].bitcast(U32), ACT.Exp, bias=guess_a[:], scale=-LN2_PER_BIT)
        nc.scalar.activation(ratio[:], sum_b[:], ACT.Copy, scale=inv_a[:])
        nc.scalar.activation(
            series[:, TERMS - 1 :],
            sum_b[:].bitcast(U32),
            ACT.Identity,
            bias=half_guess_a[:],
            scale=-0.5 * LN2_PER_BIT,
        )
        nc.scalar.activation(rest[:], undo[:].to_broadcast([P, TERMS]), ACT.Identity, bias=-1.0, scale=ratio[:])
        nc.scalar.activation(neg_inv_a[:], inv_a[:], ACT.Copy, scale=-1.0)
        nc.vector.tensor_tensor_scan(horner[:], rest[:], series[:], 0.5 / TERMS, ALU.mult, ALU.add)

        tanh = tile("tanh", [P, I], F32)
        share2 = tile("share2", [P, I], F32)
        nc.scalar.activation(tanh[:], diff[:], ACT.Tanh, bias=horner[:, TERMS - 1 :], scale=0.5)
        nc.scalar.activation(share2[:], tanh[:], ACT.Square, bias=0.5, scale=0.5)

        sized = tile("sized", [P, I], F32, tag="undo")
        cw = tile("cw", [P, I], F32)
        first = tile("first", [P, I], F32)
        second = tile("second", [P, I], F32)
        total = column("total")
        size_row = size_ps[:].rearrange("p j n -> p n j")
        for h, cols in enumerate(HALVES):
            nc.vector.scalar_tensor_tensor(
                sized[:, cols].rearrange("p (n j) -> p n j", j=PACK),
                pa[:, cols].rearrange("p (n j) -> p n j", j=PACK),
                inv_a[:],
                size_row[:, h * P // 2 : (h + 1) * P // 2, :],
                ALU.mult,
                ALU.mult,
            )
        for cols in HALVES:
            nc.vector.tensor_tensor(cw[:, cols], c_ps[:, cols], sized[:, cols], ALU.mult)
        nc.vector.scalar_tensor_tensor(first[:], share2[:], 1024.0, cw[:], ALU.mult, ALU.mult, accum_out=total[:])
        nc.vector.tensor_scalar(second[:], pa[:], total[:], neg_inv_a[:], ALU.mult, ALU.mult)
        nc.vector.tensor_tensor(gf[:].indirect(offsets[:]), first[:], second[:], ALU.add)

        start = 0
        for n, width in enumerate(CHUNKS):
            cols = slice(start, start + width)
            y = tile("y%d" % n, [P, width], F32)
            nc.vector.tensor_tensor(y[:], gf[:, cols], old_sb[:, cols], ALU.add)
            (nc.sync if n % 2 == 0 else nc.scalar).dma_start(out=out[:, cols], in_=y[:])
            start = start + width
